import numpy as np, ml_dtypes
CORES = [15,31,47,63,79,95,111,127]
N = 8
def setup_inputs(rng):
    return {"x": rng.standard_normal((N, 128, 256), dtype=np.float32).astype(ml_dtypes.bfloat16)}
def reference(x):
    s = x.sum(axis=0, dtype=np.float64).astype(x.dtype)
    p = 128 // N
    return {"y": np.stack([s[r * p:(r + 1) * p, :] for r in range(N)])}

@@ -1,0 +1,46 @@
+from concourse.bass import DstId, RemoteDMATransfer
+
+N = 8
+SCRATCH = {
+    "stage": ("dram", [N, 128, 32], "bfloat16"),
+    "land": ("dram", [N, 128, 32], "bfloat16"),
+    "res": ("dram", [128, 32], "bfloat16"),
+}
+SEMAPHORES = ["loaded", "sent", "arrived", "folded", "stored"]
+
+
+def helper_of(c):
+    return c - 1
+
+
+def rank_program(g, core, T, topo):
+    rank = T.rank_of(core)
+    if rank is not None:
+        g.dma_start(T.stage[:], T.x[:]).then_inc(T.sem.loaded, 16)
+        g.wait_ge(T.sem.loaded, 16)
+        transfers = []
+        eng = 0
+        for j in range(N):
+            h = helper_of(T.cores[j])
+            rid, pid, _se = topo.addr(h)
+            if j == rank:
+                m = 0xFF00
+            else:
+                m = 1 << eng
+                eng += 1
+            transfers.append(RemoteDMATransfer(dst_ids=[DstId(rid=rid, pnc=pid)], dma_engine_mask=m,
+                                               remote_sem=T.sem.arrived, src=T.stage[j], dst=T.land[rank]))
+        g.remote_dma_fused(transfers, local_sem=T.sem.sent)
+        g.wait_ge(T.sem.folded, 16)
+        g.dma_start(T.y[:], T.res[:]).then_inc(T.sem.stored, 16)
+        g.wait_ge(T.sem.sent, 7 + 8)
+        g.wait_ge(T.sem.stored, 16)
+        return
+    owner = core + 1
+    if T.rank_of(owner) is not None and topo.chip(owner) == topo.chip(core):
+        rid, pid, _se = topo.addr(owner)
+        g.wait_ge(T.sem.arrived, 7 + 8)
+        g.remote_dma_fused([RemoteDMATransfer(dst_ids=[DstId(rid=rid, pnc=pid)], dma_engine_mask=0xFFFF,
+                                              remote_sem=T.sem.folded, srcs=[T.land[i] for i in range(N)],
+                                              dsts=[T.res[:]], alu_op=1)], local_sem=T.sem.sent)
+        g.wait_ge(T.sem.sent, 16)

@@ -21,8 +21,7 @@ def rank_program(g, core, T, topo):
         transfers = []
         eng = 0
         for j in range(N):
-            h = helper_of(T.cores[j])
-            rid, pid, _se = topo.addr(h)
+            rid, pid, _se = topo.addr(helper_of(T.cores[j]))
             if j == rank:
                 m = 0xFF00
             else:

from concourse.bass import DstId, RemoteDMATransfer

N = 8
SCRATCH = {
    "stage": ("dram", [N, 128, 32], "bfloat16"),
    "land": ("dram", [N, 128, 32], "bfloat16"),
    "res": ("dram", [128, 32], "bfloat16"),
}
SEMAPHORES = ["loaded", "sent", "arrived", "folded", "stored"]


def helper_of(c):
    return c - 1


def rank_program(g, core, T, topo):
    rank = T.rank_of(core)
    if rank is not None:
        g.dma_start(T.stage[:], T.x[:]).then_inc(T.sem.loaded, 16)
        g.wait_ge(T.sem.loaded, 16)
        transfers = []
        eng = 0
        for j in range(N):
            rid, pid, _se = topo.addr(helper_of(T.cores[j]))
            if j == rank:
                m = 0xFF00
            else:
                m = 1 << eng
                eng += 1
            transfers.append(RemoteDMATransfer(dst_ids=[DstId(rid=rid, pnc=pid)], dma_engine_mask=m,
                                               remote_sem=T.sem.arrived, src=T.stage[j], dst=T.land[rank]))
        g.remote_dma_fused(transfers, local_sem=T.sem.sent)
        g.wait_ge(T.sem.folded, 16)
        g.dma_start(T.y[:], T.res[:]).then_inc(T.sem.stored, 16)
        g.wait_ge(T.sem.sent, 7 + 8)
        g.wait_ge(T.sem.stored, 16)
        return
    owner = core + 1
    if T.rank_of(owner) is not None and topo.chip(owner) == topo.chip(core):
        rid, pid, _se = topo.addr(owner)
        g.wait_ge(T.sem.arrived, 7 + 8)
        g.remote_dma_fused([RemoteDMATransfer(dst_ids=[DstId(rid=rid, pnc=pid)], dma_engine_mask=0xFFFF,
                                              remote_sem=T.sem.folded, srcs=[T.land[i] for i in range(N)],
                                              dsts=[T.res[:]], alu_op=1)], local_sem=T.sem.sent)
        g.wait_ge(T.sem.sent, 16)
